import numpy as np, ml_dtypes
CORES = [3,7,11,15,131,135,139,143]
N = 8
import mx_ref
BF = ml_dtypes.bfloat16
def gentries(a):
    return np.ascontiguousarray(a.reshape(8, 16, -1).transpose(0, 2, 1)).reshape(8, -1)
def gtable(e):
    e = np.asarray(e); return np.ascontiguousarray(e.reshape(8, -1, 16).transpose(0, 2, 1)).reshape(128, -1).astype(np.int32)
def gcols(t, e):
    v = np.concatenate([t.reshape(8, 16, -1, 4), np.zeros((8, 16, 1, 4), BF)], axis=2)
    return np.ascontiguousarray(np.stack([v[g][:, e[g]] for g in range(8)])).reshape(128, -1)
def tile(rs):
    return np.stack(rs, axis=2).reshape(128, -1).astype(BF)
def cut(t, i, w=512):
    return t[:, w * i:w * i + w]
def pick(q, e):
    c = np.concatenate([q[0].reshape(128, -1, 4), np.zeros((128, 1, 4), np.uint8)], axis=1); s = np.concatenate([q[1], np.ones((16, 1), np.uint8)], axis=1)
    return (np.ascontiguousarray(c[:, e].reshape(128, -1)), np.ascontiguousarray(s[:, e]))
def join(*qs):
    return (np.concatenate([q[0] for q in qs], axis=1), np.concatenate([q[1] for q in qs], axis=1))
def put(q, e, v):
    c, s = q[0].reshape(128, -1, 4).copy(), q[1].copy(); c[:, e] = v[0].reshape(128, -1, 4); s[:, e] = v[1]
    return (c.reshape(128, -1), s)
def pk(c, s):
    return (np.ascontiguousarray(c), mx_ref.live(s))
def emit(q):
    return q[0], q[1]
def packed(v, rng):
    q = [mx_ref.quantize(np.ascontiguousarray(v[r])) for r in range(N)]
    return np.stack([a for a, b in q]), np.stack([mx_ref.plane(b, rng) for a, b in q])
def values_of_codes():
    e, c = np.zeros((128, 128, 4), np.float32), np.zeros((128, 2, 4), np.uint8)
    e[np.arange(128), np.arange(128), 0] = 1
    c[:127, :, 0] = np.arange(256).reshape(2, 128).T[:127]
    return mx_ref.matmul(mx_ref.quantize(e.reshape(128, 512).astype(BF)), (c.reshape(128, 8), np.full((16, 2), 127, np.uint8))).T.reshape(-1).astype(np.float64)
CODE_VALUE, SCALE_VALUE = values_of_codes(), 2.0 ** (np.arange(256) - 127.0)
def decode(q):
    return (CODE_VALUE[q[0]].reshape(16, 8, -1, 4) * SCALE_VALUE[q[1]][:, None, :, None] + 0.0).reshape(128, -1).astype(np.float32)
def f(rng, *shape):
    return mx_ref.flush((rng.standard_normal(shape, dtype=np.float32) * np.exp2(rng.integers(-2, 3, shape[:-1] + (1,)))).astype(BF))
def wide(rng, *shape, cols=0):
    v = rng.standard_normal(shape, dtype=np.float32) * np.exp2(rng.integers(-12, 13, shape)).astype(np.float32)
    if cols: v *= np.repeat(np.exp2(rng.integers(-cols, cols + 1, shape[:-2] + (1, shape[-1] // 4))) * (rng.random(shape[:-2] + (1, shape[-1] // 4)) > 0.0625), 4, axis=-1).astype(np.float32)
    return mx_ref.flush(v.astype(BF))
C, T, S, R = 352, 32, 6, 3
STEP = [1, 2, 4]
def spines(root, right):
    n = np.concatenate([right, np.full((8, 1), C)], axis=1)
    s = [root]
    for i in range(S - 1): s.append(np.take_along_axis(n, s[-1], axis=1))
    return np.stack(s, axis=2).reshape(8, T * S)
def gput(t, e, h):
    a, b = np.concatenate([t.reshape(8, 16, -1, 4), np.zeros((8, 16, 1, 4), BF)], axis=2), h.reshape(8, 16, -1, 4)
    for g in range(8): a[g][:, e[g]] = b[g]
    return np.ascontiguousarray(a[:, :, :C]).reshape(128, -1)
def big(v):
    v = v.astype(np.float32)
    v[np.abs(v) < np.float32(2.0 ** -16)] = 0
    return v.astype(BF)
def numbers_of(rng):
    return {"x": big(f(rng, N, 128, 4 * C)), "u": np.array(f(rng, N, 128, 512)), "v": np.array(f(rng, N, 128, 512))}
def layers(rng):
    return big(f(rng, N, 128, 2048)).reshape(N, 8, 16, 4, 8, 16, 4)
def weights(rng, w):
    c, p = packed(np.ascontiguousarray(w).reshape(N, 128, 2048), rng)
    return {"wc": c, "ws": p}
def signs(rng):
    return rng.permutation(8) % 2 * 2.0 - 1.0
def shape(rng, own, chance, plan=()):
    left, right, n = [C] * C, [C] * C, T
    def hang(h, side, k):
        nonlocal n
        for _ in range(k):
            side[h] = n
            h, side, n = n, right, n + 1
    for m, (a, b, c) in enumerate(plan):
        hang(m, right, a - 1)
        if a > S: hang(n - 1, left, 1)
        hang(m, left, b - 1)
        hang(right[m], left, c - 2)
    way, tree = (rng.random((C, 16)) < chance[own][:, None]).tolist(), own.tolist()
    for j in range(n, C):
        h, i, side = tree[j], 0, (left, right)[way[j][0]]
        while side[h] < C:
            h, i = side[h], i + 1
            side = (left, right)[way[j][i % 16]]
        side[h] = j
    return left, right
def grown(rng):
    return shape(rng, rng.integers(0, T, C), rng.choice([0.3, 0.6, 0.8, 0.95], T))
def places(rng):
    return np.argsort(rng.random((N, 8, C)), axis=2)
def links(e, a):
    t = np.zeros((2, N, 8, C), np.int64)
    for r in range(N):
        for g in range(8):
            p = np.append(e[r, g], C)
            for i in range(2): t[i, r, g, e[r, g]] = p[a[r][g][i]]
    return {"ro": np.stack([gtable(e[r, :, :T]) for r in range(N)]), "le": np.stack([gtable(q) for q in t[0]]), "ri": np.stack([gtable(q) for q in t[1]])}
def forests(rng):
    return links(places(rng), [[grown(rng) for g in range(8)] for r in range(N)])
def setup_inputs(rng):
    return {**numbers_of(rng), **weights(rng, layers(rng)), **forests(rng)}
def setup_inputs_ties(rng):
    d = numbers_of(rng)
    e = rng.permutation(N)
    x = d["x"].reshape(N, 8, 16, C, 4)
    a = x[0][:, :8, :3].copy()
    a[:, :, 2] = 0
    for r in range(N):
        k = np.zeros(C, int) if r == e[0] else rng.permutation(C) % 3
        x[r][:, :8] = a[:, :, k]
    x[e[1]][:, :8] = 0
    u = d["u"].reshape(N, 8, 16, 8, 16, 4)
    k = u[0].copy()
    u[:, :, :, :, 0] = 0
    for g in range(8): u[:, g, :8, g, 0] = k[g, :8, g, 0]
    w = layers(rng)
    w[:, :, :, :, :, :8] = 0
    return {"x": x.reshape(N, 128, 4 * C), "u": u.reshape(N, 128, 512), "v": d["v"], **weights(rng, w), **forests(rng)}
def setup_inputs_near(rng):
    d = numbers_of(rng)
    k = forests(rng)
    x = np.zeros((N, 8, 16, C, 4), np.float32)
    u = d["u"].reshape(N, 128, 128, 4)
    u[:, :, ::16] = 0
    c, half = signs(rng), int(rng.integers(2))
    for r in range(N):
        low, up = 2 * r // N == half, int((r & STEP[0]) > 0)
        root = gentries(k["ro"][r])
        i = rng.integers(0, S, (8, C + 1))
        np.put_along_axis(i, spines(root, gentries(k["ri"][r])), np.arange(T * S)[None] % S, axis=1)
        s = (i[:, :C] + 1 + (0 if low else S * up)) // 2
        size = 2.0 ** -6 if low else 1.0
        x[r, :, 0, :, 0] = ((8 * c + up) * 2.0 ** -30 if low else c)[:, None]
        x[r, :, 8] = ((s[:, :, None] >> np.arange(4)) & 1) * np.exp2(np.arange(4) - 23.0) * size
        x[r, :, 10:] = rng.integers(4, 8, (8, 6, C, 4)) * 2.0 ** -20 * size
        if not low:
            for g in rng.permutation(8)[:4]: x[r, g, 0, root[g, rng.integers(T)], 0] *= np.float32(2.0 ** 30)
        for h in range(0, 128, 16):
            u[r, h, h, 0] = 2.0 ** -30 if low else 1.0
            u[r, h + 8, h] = 2.0 ** -30 if low else 1.0
    w = layers(rng)
    w[:, :, :10] = 0
    w[:, :, :, :, :, :10] = 0
    return {"x": x.reshape(N, 128, 4 * C).astype(BF), "u": u.reshape(N, 128, 512), "v": d["v"], **weights(rng, w), **k}
def setup_inputs_huge(rng):
    d = numbers_of(rng)
    e, a = places(rng), [grown(rng) for r in range(N)]
    x = 0.6 + 0.2 * rng.random((N, 8, 16, C, 4))
    half = int(rng.integers(2))
    for r in range(N):
        c = rng.permutation(C) % 2 if 2 * r // N != half else np.zeros(C, int)
        for g in range(8): x[r, g][:, e[r, g]] *= np.where(c > 0, 2.0 ** 29, -2.0 ** 30)[None, :, None]
    u = d["u"].reshape(N, 128, 128, 4)
    k = 2.0 ** 30 * (1 - 0.25 * rng.random((N, 128, 8, 4))) * signs(rng)[None, None, :, None]
    u[:, :, ::16] = k.astype(np.float32).astype(BF)
    w = np.zeros((N, 128, 4, 128, 4), np.float32)
    i = np.arange(128)
    for b in range(4): w[:, i, b, i, b] = 4
    return {"x": x.astype(np.float32).reshape(N, 128, 4 * C).astype(BF), "u": u.reshape(N, 128, 512), "v": d["v"], **weights(rng, w.astype(BF)), **links(e, [[a[r]] * 8 for r in range(N)])}
def setup_inputs_slots(rng):
    n = [(S + 1,) * 3] * 2 + [(S,) * 3] * 2 + [(S - 1,) * 3] + [(1, 1, 1)] * 3 + [(1, S, 1), (S, 1, 2)]
    h = rng.permutation(8)
    a = []
    for r in range(N):
        odd = bin(r).count("1") % 2
        a.append([])
        for g in range(8):
            o = rng.permutation(10)
            if g == h[0]: o = np.arange(10)
            if g == h[1]: o = (np.arange(10) + 5 * odd) % 10
            a[r].append(shape(rng, rng.integers(10, T, C), rng.choice([0.3, 0.6, 0.8, 0.95], T), [n[i] for i in o]))
    return {**numbers_of(rng), **weights(rng, layers(rng)), **links(places(rng), a)}
def setup_inputs_spread(rng):
    d = setup_inputs(rng)
    d["x"] = big(wide(rng, N, 128, 4 * C, cols=6))
    return d
def check_inputs(d):
    b = []
    for k in ("x", "u", "v"):
        a = np.abs(d[k].astype(np.float32))
        if not (np.isfinite(a).all() and ((a == 0) | (a >= 2.0 ** -30) & (a <= 2.0 ** 30)).all()): b.append("a value of " + k)
    none, least, most = [emit(mx_ref.quantize(np.full((128, 16), k, np.float32).astype(BF)))[1][0, 0] for k in (0.0, 2.0 ** -30, 2.0 ** 30)]
    for r in range(N):
        if ((d["wc"][r] == 0x7F) | (d["wc"][r] == 0xFF)).any(): b.append("wc: a code that is no number")
        s = mx_ref.live(d["ws"][r])
        if ((s != none) & ((s < least) | (s > most))).any(): b.append("ws: a scale out of range")
        root, left, right = [gentries(d[k][r]) for k in ("ro", "le", "ri")]
        if (root < 0).any() or (root >= C).any() or (left < 0).any() or (left > C).any() or (right < 0).any() or (right > C).any():
            b.append("an entry of ro, le or ri out of range")
            continue
        for g in range(8):
            k = np.bincount(np.concatenate([root[g], left[g], right[g]]), minlength=C + 1)
            if (k[:C] != 1).any(): b.append("a place that isn't once a root or a child")
            up = np.arange(C + 1)
            up[left[g]] = np.arange(C)
            up[right[g]] = np.arange(C)
            up[root[g]] = root[g]
            up[C] = C
            for i in range(10): up = up[up]
            if not np.isin(up[:C], root[g]).all(): b.append("a place that no root reaches")
    return b
def reference(x, u, v, wc, ws, ro, le, ri):
    qu = [mx_ref.quantize(u[r]) for r in range(N)]
    lay = [pk(wc[r], ws[r]) for r in range(N)]
    now = [x[r] for r in range(N)]
    root, left, right = [[gentries(a[r]) for r in range(N)] for a in (ro, le, ri)]
    for t in range(R):
        s, sent, score = [], [], []
        for r in range(N):
            s.append(spines(root[r], right[r]))
            sent.append(mx_ref.quantize(gcols(now[r], s[r])))
            score.append(mx_ref.matmul(qu[r], sent[r])[::16].reshape(8, T, S))
        came = decode(join(*sent)).astype(BF)
        for r in range(N):
            lo, hi = min(r, r ^ STEP[t]), max(r, r ^ STEP[t])
            full = [(s[i] < C).reshape(8, T, S) for i in (lo, hi)]
            key = np.concatenate([score[lo], score[hi]], axis=2) + np.float32(0.0)
            o = np.lexsort((-key, ~np.concatenate(full, axis=2)), axis=2)
            first = np.sum(full[0], axis=2, keepdims=True) * int(r == hi)
            a = np.take_along_axis(o, first + np.arange(S), axis=2)
            a = a // S * (T * S) + S * np.arange(T)[:, None] + a % S
            a = np.where(full[int(r == hi)], a, -1)
            n = np.concatenate([a[:, :, 1:], np.full((8, T, 1), -1)], axis=2)
            n = np.where(n < 0, a, n)
            both = np.concatenate([cut(came, lo, 4 * T * S), cut(came, hi, 4 * T * S)], axis=1)
            e = gcols(both, a.reshape(8, -1)).astype(np.float32)
            z = ((e + gcols(both, n.reshape(8, -1)).astype(np.float32)) * np.float32(0.5)).astype(BF)
            q = mx_ref.quantize(z)
            h = tile([np.maximum(mx_ref.matmul(pick(lay[r], np.arange(128 * b, 128 * b + 128)), q), np.float32(0.0)) * np.float32(0.03125) + e[:, b::4] for b in range(4)])
            now[r] = gput(now[r], s[r], h)
            m = np.zeros((8, C + 1), bool)
            np.put_along_axis(m, s[r], True, axis=1)
            m = m[:, :C]
            left[r], right[r] = np.where(m, right[r], left[r]), np.where(m, left[r], right[r])
    y, ol = np.zeros((N, 128, C), np.float32), np.zeros((N, 8, 2 * C), np.float32)
    oc, osc = np.zeros((N, 128, 4 * C), np.uint8), np.zeros((N, 16, C), np.uint8)
    for r in range(N):
        q = mx_ref.quantize(now[r])
        y[r] = mx_ref.matmul(mx_ref.quantize(v[r]), q)
        ol[r] = np.concatenate([left[r], right[r]], axis=1)
        oc[r], osc[r] = emit(q)
    return {"y": y, "ol": ol, "oc": oc, "osc": osc}

from concourse.bass import DstId, RemoteDMATransfer
from concourse.mybir import dt, AluOpType as OP, ActivationFunctionType as AF

C = 352
STEP = [1, 2, 4]
CP = 368
F32, BF, I32, U16, X4, U8 = "float32", "bfloat16", "int32", "uint16", "float8_e4m3fn_x4", "uint8"
SIZE = {F32: 4, BF: 2, I32: 4, U16: 2, X4: 4, U8: 1}
DW = [560, 400, 400]
FW = 880
ROUND = 12582912.0
CY, GATHER, SCATTER, SYNC, CALL, FAR, FIRST = 1.0, 1.55, 3.5, 90.0, 500.0, 1700.0, 2000.0
TRIES, HEAT, WEIGHT, LOAD, SEED = 5000, 30.0, 0.1, 0.3, 1
PLAN = []
EST = []


def _scratch():
    s = {}

    def sb(names, n, d):
        for k in names.split():
            s[k] = ("sbuf", [128, n], d)
    sb("W0", 2 * CP, I32); sb("RO", 8, I32); sb("RIW", 24, I32); sb("PI", 8, I32); sb("CI", 8, I32); sb("QI", 96, I32)
    sb("CF", 40, F32); sb("C16", 32, F32); sb("J", 32, F32); sb("TMP", 512, F32); sb("LF", 16, F32)
    sb("TB", 4 * CP, F32); sb("ROW", 960, F32); sb("TT", 1024, F32); sb("PL", 48, F32)
    sb("POS RI16 FO", 24, U16); sb("OLO", 44, U16); sb("LS", 16, U16); sb("OA OB OC OD", 16, U16); sb("XO", 64, U16); sb("XO2", 80, U16)
    sb("LT", 86, U16); sb("AO NO", 36, U16); sb("SCO", 30, U16); sb("OZ", 2, U16)
    sb("XS", 4 * C + 16, BF); sb("US VS", 512, BF); sb("ONE EYE", 516, BF)
    sb("QX LQX QF", C, X4); sb("SX LSX SF", C, U8)
    sb("QU QV", 128, X4); sb("SU SV", 128, U8); sb("QE QW", 512, X4); sb("SE SW", 512, U8)
    sb("B0", 4 * 224, BF); sb("QB0", 224, X4); sb("SB0", 224, U8)
    sb("B1 B2", 4 * 192, BF); sb("QB1 QB2", 384, X4); sb("SB1 SB2", 384, U8)
    sb("BD", 512, BF); sb("QD1 QD2", 128, X4); sb("SD1 SD2", 128, U8)
    sb("TS", 416 + 2 * 352 + 2 * 96, F32); sb("SK0 SK1 SK2", 32, F32); sb("OUT0 OX1 OX2 LPL", 16, F32); sb("LX1 LX2", 8, F32)
    sb("OS1 OS2 LS1 LS2", 40, F32); sb("CAP", 96, F32); sb("FL", 48, F32)
    sb("G1 CM ST D0C", 288, F32); sb("K12 TGH TG2 NQ SC", 144, F32); sb("TG", 432, F32); sb("DB", 288, F32); sb("CC", 32, F32); sb("IDS DL", 64, F32)
    sb("D0", 4 * DW[0], BF); sb("D1 D2", 4 * DW[1], BF); sb("RL", 3 * 768, F32); sb("EH EG", 3 * 768, BF)
    sb("ZC", 512, BF); sb("ZR", 3 * 768, BF); sb("QZC", 128, X4); sb("SZC", 128, U8); sb("QZR", 3 * 192, X4); sb("SZR", 3 * 192, U8)
    sb("FP", 4 * FW, BF); sb("XF", 4 * C, BF); sb("M", 848, F32); sb("VAL", 480, F32); sb("MT", 736, F32)
    sb("OLR", 2 * C, F32); sb("YS", C, F32)
    s["PA"] = ("psum", [128, 2048], F32)
    s["PB"] = ("psum", [128, 2048], F32)
    return s


SCRATCH = _scratch()
ARR = ["aqx", "asx", "apl", "as0", "ac1", "as1", "ad1", "ax1", "ac2", "as2", "ad2", "ax2"]
SEMAPHORES = ["cv", "cs", "ct", "cg", "sent"] + ARR + ["d%d" % i for i in range(24)]


def V(n, a, b, s=1):
    return (n, a, b, s)


def ind(w, o):
    return ("ind", w, o)


def regs(x):
    if x[0] == "ind":
        return regs(x[1]) + regs(x[2])
    n, a, b, s = x
    z = SIZE[SCRATCH[n][2]]
    if SCRATCH[n][0] == "psum":
        return [(n, a // 512 * 2048, (b + 511) // 512 * 2048, 1, 0)]
    return [(n, a * z, b * z, s, a % s)]


def meet(r, w, dma, r2, w2, dma2, other):
    n, a, b, s, ph = r
    n2, a2, b2, s2, ph2 = r2
    if not (w or w2 or (other and SCRATCH[n][0] == "psum")):
        return False
    if w and w2 and dma != dma2:
        return a // 16 < (b2 + 15) // 16 and a2 // 16 < (b + 15) // 16
    return a < b2 and a2 < b and not (s == s2 and s > 1 and ph != ph2)


def count(x):
    if x[0] == "ind":
        return 16 * count(x[2])
    return (x[2] - x[1] + x[3] - 1) // x[3]


def kind(x):
    return SCRATCH[(x[1] if x[0] == "ind" else x)[0]][2]


def lay_out(ops):
    seen = {}
    for i, o in enumerate(ops):
        dep = set(o["after"]) | set(o.get("behind", ()))
        for r, w in o["acc"]:
            for j, r2, w2 in seen.get(r[0], []):
                if j != i and meet(r, w, o["dma"], r2, w2, ops[j]["dma"], len(o["alt"]) > 1 or o["alt"].keys() != ops[j]["alt"].keys()):
                    dep.add(j)
            seen.setdefault(r[0], []).append((i, r, w))
        o["dep"] = dep
    way = [0.0] * len(ops)
    for i in range(len(ops) - 1, -1, -1):
        way[i] += min(c for c, f in ops[i]["alt"].values()) + ops[i]["lat"] + SYNC
        for j in ops[i]["dep"]:
            way[j] = max(way[j], way[i])
    tail = [o["lat"] + SYNC for o in ops]
    deps = [sorted(o["dep"]) for o in ops]
    alts = [[(q, c) for q, (c, f) in o["alt"].items()] for o in ops]
    marks = [i for i, o in enumerate(ops) if o["what"] == "land"]

    def sweep(key, pick):
        held, at = {}, [None] * len(ops)
        eff = [key[i] for i in range(len(ops))]
        for i in range(len(ops) - 1, -1, -1):
            e = eff[i] + 0.01
            for j in deps[i]:
                if eff[j] < e:
                    eff[j] = e
        last, load = (0.0, 0), 0.0
        for i in sorted(range(len(ops)), key=lambda k: -eff[k]):
            t, why = 0.0, -1
            for j in deps[i]:
                if at[j][0] + tail[j] > t:
                    t, why = at[j][0] + tail[j], j
            q, c = alts[i][pick[i]]
            h, n = held.setdefault(q, []), 0
            if q:
                for a, b, j in h:
                    if t + c <= a:
                        break
                    n += 1
                    if b > t:
                        t, why = b, j
                h.insert(n, (t, t + c, i))
            at[i] = (t + c, t, q, why)
            if t + c + tail[i] > last[0]:
                last = (t + c + tail[i], i)
            if q == "v":
                load += c
        return last, at, last[0] + WEIGHT * sum(at[i][0] for i in marks) + LOAD * load

    if not PLAN:
        seed = [SEED]

        def rnd(n):
            seed[0] = (seed[0] * 1103515245 + 12345) % 2147483648
            return (seed[0] >> 8) % n
        key = dict(enumerate(way))
        pick = [len(a) - 1 for a in alts]
        last, at, val = sweep(key, pick)
        best = (last, at, key, pick, val)
        for n in range(TRIES):
            chain, i = [], last[1] if rnd(2) else marks[rnd(len(marks))]
            while at[i][3] >= 0:
                if at[i][3] not in deps[i]:
                    chain.append((i, at[i][3]))
                i = at[i][3]
            k2, p2 = dict(key), list(pick)
            for m in range(1 + rnd(2)):
                i, j = chain[rnd(len(chain))] if chain else (rnd(len(ops)), rnd(len(ops)))
                move = rnd(8)
                if move > 5:
                    some = [x for x in range(len(ops)) if not p2[x] and len(alts[x]) > 1]
                    if some:
                        x = some[rnd(len(some))]
                        p2[x] = 1 + rnd(len(alts[x]) - 1)
                elif move < 2 and len(alts[(i, j)[move]]) > 1:
                    p2[(i, j)[move]] = (p2[(i, j)[move]] + 1) % len(alts[(i, j)[move]])
                elif move == 2:
                    k2[j] = k2[i] - 1 - rnd(500)
                elif move == 3:
                    k2[i] = k2[j] + 1 + rnd(500)
                else:
                    up, todo = 500 + rnd(8000), [j]
                    for d in range(4):
                        for x in todo:
                            k2[x] = max(k2[x], key[j] + up)
                        todo = sorted(set(y for x in todo for y in deps[x]))
            l2, a2, v2 = sweep(k2, p2)
            if v2 <= val + HEAT * (1 - n / TRIES):
                last, at, val, key, pick = l2, a2, v2, k2, p2
                if val < best[4]:
                    best = (last, at, key, pick, val)
        PLAN.extend([{i: -a[1] for i, a in enumerate(best[1])}, best[3]])
    last, at, val = sweep(PLAN[0], PLAN[1])
    for o, a in zip(ops, at):
        o["end"], o["start"], o["q"] = a[:3]
    EST.append((round(last[0]), round(max(way))))
    return sorted(range(len(ops)), key=lambda k: (ops[k]["start"], k))


def rank_program(g, core, T, topo):
    rank = T.rank_of(core)
    if rank is None:
        return
    Q = {"v": g.vector, "s": g.scalar, "t": g.tensor, "g": g, "y": g.sync}
    ops = []

    def ap(x):
        if x[0] == "ind":
            return ap(x[1]).indirect(ap(x[2]))
        n, a, b, s = x
        return T[n][:, a:b:s] if s != 1 else T[n][:, a:b]

    def raw(x):
        return ap(x).bitcast(dt.uint8) if kind(x) == X4 else ap(x)

    def add(what, alt, rd, wr, lat=0.0, after=(), **more):
        acc = [(r, False) for x in rd if isinstance(x, tuple) for r in regs(x)] + [(r, True) for x in wr for r in regs(x)]
        ops.append(dict(what=what, alt=alt, acc=acc, lat=lat, after=list(after), dma=what != "op", **more))
        return len(ops) - 1

    def cost(o, *i, two=False):
        n = count(o)
        if any(x[0] == "ind" for x in i if isinstance(x, tuple)):
            return 55 + n * GATHER * CY
        if all(SIZE[kind(x)] == 2 for x in (o,) + i if isinstance(x, tuple)) and not two:
            n = n / 2
        return max(64, n * (2 if two else 1)) * CY

    def scost(o, i):
        return 65 + count(o) * CY * (GATHER if i[0] == "ind" else 1)

    def sc(x):
        return ap(x) if isinstance(x, tuple) else x
    flo = lambda *x: all(kind(k) in (F32, BF) for k in x)

    def dma(q, rd, wr, out, in_, lat, after=()):
        return add("dma", {k: (60.0, lambda e: e.dma_start(out, in_)) for k in q}, rd, wr, lat, after)

    first, opened = [FIRST], []

    def send(t, sem, pairs, land=None):
        dst = T.cores[rank ^ STEP[t]]
        rid, pid = topo.addr(dst, core)
        eng = topo.engines(core, dst)
        k = len(eng) // len(pairs)

        def call(e):
            if len(pairs) == 1:
                return e.remote_dma(raw(pairs[0][1]), raw(pairs[0][0]), T.sem[sem], T.sem.sent, pid, rid, topo.mask(core, dst))
            return e.remote_dma_fused([RemoteDMATransfer(dst_ids=[DstId(rid=rid, pnc=pid)], dma_engine_mask=sum(1 << z for z in eng[k * i:k * i + k]),
                                                         remote_sem=T.sem[sem], src=raw(p[0]), dst=raw(p[1])) for i, p in enumerate(pairs)], local_sem=T.sem.sent)
        i = add("send", {"g": (CALL + first[0], call)}, [p[0] for p in pairs], [], n=k * len(pairs), behind=opened[:1])
        opened.append(i)
        back = len(topo.engines(dst, core)) // len(pairs) * len(pairs)
        lat = FAR + 128 / k * (30 + count(pairs[0][0]) * SIZE[kind(pairs[0][0])] / 20)
        first[0] = 0.0
        add("land", {"": (1.0, None)}, [], land or [p[1] for p in pairs], lat, [i], sem=sem, n=back)

    def fill(o, pat, base, cm):
        if kind(o) == I32:
            return (130 + 2 * CY * count(o), lambda q: q.iota(ap(o), pat, base, cm))
        return (130 + 2 * CY * count(o), lambda q: q.iota(ap(o), pat, base, cm, allow_small_or_imprecise_dtypes=True))

    def iota(o, pat, base, cm=0):
        add("op", {"g": fill(o, pat, base, cm)}, [], [o])

    def mem(o, c, g_=True):
        alt = {"v": (cost(o), lambda q: q.memset(ap(o), c))}
        if kind(o) != U16 and o[3] == 1 and abs(c) < 256 and g_:
            alt["g"] = fill(o, [[0, count(o)]], int(c), 0)
        return add("op", alt, [], [o])

    def cp(o, i, g_=False):
        alt = {"v": (cost(o, i), lambda q: q.tensor_copy(ap(o), ap(i)))}
        if flo(o, i):
            alt["s"] = (scost(o, i), lambda q: q.activation(ap(o), ap(i), AF.Copy))
        if g_:
            alt["g"] = (170 + 2 * CY * count(o), lambda q: q.affine_select(ap(o), ap(i), [[0, count(o)]], OP.is_equal, 0.0, 0, 0))
        add("op", alt, [i], [o])

    def tt(o, a, b, f):
        add("op", {"v": (cost(o, a, two=True), lambda q: q.tensor_tensor(ap(o), ap(a), ap(b), f))}, [a, b], [o])

    def ts(o, a, s1, f1, s2=None, f2=None):
        if f2 is None:
            alt = {"v": (cost(o, a), lambda q: q.tensor_scalar(ap(o), ap(a), sc(s1), None, f1))}
        else:
            alt = {"v": (cost(o, a), lambda q: q.tensor_scalar(ap(o), ap(a), sc(s1), sc(s2), f1, f2))}
        if flo(o, a):
            if f1 == OP.mult and f2 is None:
                alt["s"] = (scost(o, a), lambda q: q.activation(ap(o), ap(a), AF.Identity, scale=sc(s1)))
            elif f1 == OP.add and f2 is None:
                alt["s"] = (scost(o, a), lambda q: q.activation(ap(o), ap(a), AF.Identity, bias=sc(s1)))
            elif f1 == OP.mult and f2 == OP.add:
                alt["s"] = (scost(o, a), lambda q: q.activation(ap(o), ap(a), AF.Identity, scale=sc(s1), bias=sc(s2)))
            elif f1 == OP.max and s1 == 0.0 and f2 == OP.mult:
                alt["s"] = (scost(o, a), lambda q: q.activation(ap(o), ap(a), AF.Relu, scale=s2))
        add("op", alt, [a, s1, s2], [o])

    def scan(o, a, b):
        add("op", {"v": (cost(o, a), lambda q: q.tensor_tensor_scan(ap(o), ap(a), ap(b), 0.0, OP.mult, OP.add))}, [a, b], [o])

    def tr(o, i):
        add("op", {"v": (cost(o, i), lambda q: q.transpose(ap(o), ap(i)))}, [i], [o])

    def quant(c, s, a, n, i):
        c, s = V(c, a, a + n), V(s, a, a + n)
        add("op", {"v": (15 + 1.05 * n, lambda q: q.quantize_mx(ap(c), ap(s), ap(i)))}, [i], [c, s])

    def mm(p, bank, lc, ls, la, rc, rs, ra, n):
        o, w = V(p, 512 * bank, 512 * bank + n), (V(lc, la, la + 128), V(ls, la, la + 128), V(rc, ra, ra + n), V(rs, ra, ra + n))
        add("op", {"t": (30 + 0.6 * (n + 16), lambda q: q.matmul_mx(ap(o), ap(w[0]), ap(w[1]), ap(w[2]), ap(w[3]), True, True))}, w, [o])

    low = [(rank & s) == 0 for s in STEP]
    col = lambda n, k: V(n, k, k + 1)
    R_, E_, I_, H_, E16, X_, Y_ = [col("CF", k) for k in range(7)]
    LIN, DUP, STR, SEL6, SEL5, SEL1, HL = [col("LS", 2 * k) for k in range(7)]
    lf = lambda x: col("LF", x[1])
    LP, LI, LC, LSTH, LSTL = [V("LT", 36 + 10 * k, 45 + 10 * k) for k in range(5)]
    L1, R1, R2, R3 = [V("TB", CP * k, CP * k + CP) for k in range(4)]

    m0 = mem(V("W0", 0, CP), C)
    m1 = mem(V("W0", CP, 2 * CP), C)
    dma("y", [], [V("RO", 0, 2)], T.RO[:, 0:2], T.ro[:], 1800)
    dma("y", [], [V("RIW", 0, 22)], T.RIW[:, 0:22], T.ri[:], 1900)
    dma("s", [], [V("W0", 0, C)], T.W0[0:128:16, 0:C], T.ri[:], 1800)
    dma("y", [], [V("XS", 0, 4 * C)], T.XS[:, 0:4 * C], T.x[:], 3000, [m0])
    dma("s", [], [V("W0", CP, CP + C)], T.W0[0:128:16, CP:CP + C], T.le[:], 2600)
    dma("y", [], [V("US", 0, 512)], T.US[:], T.u[:], 3200, [m1])
    dma("y", [], [V("QW", 0, 512)], raw(V("QW", 0, 512)), T.wc[:], 4500, [m1])
    dma("y", [], [V("SW", 0, 512)], T.SW[:], T.ws[:], 4500, [m1])
    dma("y", [], [V("VS", 0, 512)], T.VS[:], T.v[:], 4500, [m1])

    iota(col("PI", 0), [[0, 1]], 0, 1)
    iota(V("C16", 0, 32), [[16, 32]], 0)
    mem(V("ONE", 0, 516), 1.0)
    ts(col("CI", 0), col("PI", 0), 15, OP.bitwise_and)
    ts(col("CI", 1), col("PI", 0), 4, OP.arith_shift_right, 1, OP.bitwise_and)
    ts(col("CI", 2), col("PI", 0), 1, OP.arith_shift_right, 7, OP.bitwise_and)
    ts(col("CI", 3), col("PI", 0), 1, OP.bitwise_and)
    add("op", {"g": (170 + 2 * CY * 516, lambda q: q.affine_select(ap(V("EYE", 0, 516)), ap(V("ONE", 0, 516)), [[-1, 516]], OP.is_equal, 0.0, 3, 4))},
        [V("ONE", 0, 516)], [V("EYE", 0, 516)])
    mem(V("POS", 22, 24), C)
    mem(V("RI16", 22, 24), C)
    cp(V("CF", 0, 4), V("CI", 0, 4))
    mem(V("TT", 0, 64), 0.0, False)
    mem(V("XS", 4 * C, 4 * C + 16), 0.0, False)
    ts(col("CF", 8), R_, 22.0, OP.mult)
    ts(E16, E_, 16.0, OP.mult)
    ts(col("CF", 9), R_, 11.0, OP.min, 32.0, OP.mult)
    ts(col("CF", 10), I_, 3.0, OP.min, 32.0, OP.mult)
    ts(V("POS", 0, 22), V("C16", 0, 22), 0.0625, OP.mult, col("CF", 8), OP.add)
    ts(LIN, col("CF", 9), E16, OP.add)
    ts(DUP, col("CF", 10), E16, OP.add)
    ts(V("J", 0, 32), V("C16", 0, 32), R_, OP.add)
    tt(X_, H_, E_, OP.not_equal)
    ts(col("CF", 11), E_, -32.0, OP.mult, 32.0, OP.add)
    ts(col("CF", 12), I_, 5.0, OP.min, 32.0, OP.mult)
    ts(col("CF", 13), I_, 4.0, OP.min, 32.0, OP.mult)
    ts(col("CF", 14), H_, 32.0, OP.mult, E16, OP.add)
    ts(Y_, X_, col("CF", 11), OP.mult, E16, OP.add)
    ts(col("CF", 15), X_, 192.0, OP.mult, Y_, OP.add)
    ts(col("CF", 16), X_, 160.0, OP.mult, Y_, OP.add)
    ts(col("CF", 17), X_, 352.0, OP.mult, Y_, OP.add)
    ts(col("CF", 18), I_, 2.0, OP.min, 32.0, OP.mult)
    ts(col("CF", 19), col("CF", 17), 256.0, OP.add)
    ts(SEL6, col("CF", 15), col("CF", 12), OP.add)
    mem(V("LF", 0, 16), 0.0)
    ts(STR, col("CF", 13), 4.0, OP.mult, col("CF", 14), OP.add)
    ts(lf(SEL5), col("CF", 16), col("CF", 13), OP.add)
    ts(lf(SEL1), X_, 32.0, OP.mult, Y_, OP.add)
    cp(lf(HL), H_)
    ts(col("LF", 14), I_, 32.0, OP.mult, col("CF", 17), OP.add)
    ts(col("LF", 15), col("CF", 18), col("CF", 19), OP.add)
    cp(V("LS", 8, 16), V("LF", 8, 16))
    mem(V("B0", 0, 64), 0.0, False)
    mem(V("B0", 832, 896), 0.0, False)
    iota(V("K12", 0, 144), [[0, 12], [6, 2], [-1, 6]], -5)
    iota(V("TGH", 0, 144), [[-1, 6], [0, 2], [-1, 12]], 6)
    ops[-2]["skip"], ops[-1]["skip"] = not any(low), all(low)
    tgh = len(ops) - 1
    iota(V("CF", 20, 32), [[-1, 6], [0, 2]], 11)
    iota(V("D0C", 0, 288), [[0, 288]], 1)
    mem(V("D0C", 0, 288, 25), -1.0)
    mem(V("D0C", 12, 288, 25), -1.0)
    mem(V("D0C", 0, 288, 12), 0.0)
    t_ = lambda k, n=18: V("TMP", 18 * k, 18 * k + n)
    u_ = lambda k, n=9: V("TMP", 180 + 10 * k, 180 + 10 * k + n)
    mem(V("TMP", 180, 230), 0.0)
    ts(t_(0), V("J", 0, 18), 1.0 / 12, OP.mult, -0.4583, OP.add)
    ts(t_(1), t_(0), ROUND, OP.add, ROUND, OP.subtract)
    ts(t_(2), t_(1), 0.5, OP.mult, -0.25, OP.add)
    ts(t_(3), t_(2), ROUND, OP.add, ROUND, OP.subtract)
    ts(t_(4), t_(1), -11.5, OP.mult)
    tt(t_(5), V("J", 0, 18), t_(3), OP.subtract)
    tt(t_(6), t_(5), t_(4), OP.add)
    ts(t_(7), t_(6), 2.0, OP.mult)
    tt(t_(8), t_(7), t_(1), OP.min)
    tt(t_(9), t_(7), t_(1), OP.max)
    cp(u_(0), t_(1, 9))
    cp(u_(1), t_(7, 9))
    ts(t_(0, 9), t_(7, 9), 12.0, OP.is_ge, 4.0, OP.mult)
    ts(u_(3), t_(7, 9), 12.0, OP.mult, 11.0, OP.add)
    tt(u_(2), t_(0, 9), t_(7, 9), OP.add)
    ts(t_(2, 9), t_(0, 9), -72.0, OP.mult, 144.0, OP.add)
    tt(u_(4), t_(2, 9), u_(3), OP.add)
    cp(V("LT", 0, 86), V("TMP", 144, 230))

    cp(V("RI16", 0, 22), V("RIW", 0, 22))
    cp(V("OA", 0, 4, 2), V("RO", 0, 2))
    cp(V("OA", 1, 4, 2), V("RO", 0, 2))
    cp(V("TT", 0, 64, 32), V("RO", 0, 2))
    cp(V("TT", 16, 64, 32), V("RO", 0, 2))

    def table(k, win, off, cuts):
        for a, b in cuts:
            cp(V("TB", CP * k + 16 * a, CP * k + 16 * b), ind(win, V(off, a, b)))
    table(1, V("W0", 0, CP), "POS", ((0, 23),))
    table(2, R1, "RI16", ((0, 12), (12, 23)))
    table(3, R2, "RI16", ((0, 12), (12, 23)))
    cp(V("ROW", 0, 64), ind(R1, V("OA", 0, 4)))
    cp(V("ROW", 64, 128), ind(R2, V("OA", 0, 4)))
    quant("QX", "SX", 0, C, V("XS", 0, 4 * C))
    send(0, "aqx", [(V("QX", 0, C), V("LQX", 0, C))])
    send(0, "asx", [(V("SX", 0, C), V("LSX", 0, C))])
    tr(V("TT", 64, 192), V("ROW", 0, 128))
    cp(V("OB", 0, 16), ind(V("TT", 64, 192), DUP))
    for k, w in enumerate((R1, R2, R3)):
        cp(V("ROW", 128 + 64 * k, 192 + 64 * k), ind(w, V("OB", 4, 8)))
    tr(V("TT", 192, 384), V("ROW", 128, 320))
    for t in range(4):
        ts(V("XO", 16 * t, 16 * t + 16), ind(V("TT", 0, 384), LIN), 4.0, OP.mult, float(t), OP.add)
    XW = V("XS", 0, 4 * C + 16)
    for t in range(4):
        cp(V("B0", 64 + t, 832, 4), ind(XW, V("XO", 16 * t, 16 * t + 12)))
    quant("QU", "SU", 0, 128, V("US", 0, 512))
    quant("QB0", "SB0", 0, 224, V("B0", 0, 896))
    mm("PB", 0, "QU", "SU", 0, "QB0", "SB0", 0, 224)
    cp(V("PL", 0, 16), ind(V("TT", 0, 384), LIN))
    send(0, "apl", [(V("PL", 0, 12), V("LPL", 0, 12))])
    table(0, V("W0", CP, 2 * CP), "POS", ((0, 12), (12, 23)))

    def caps(t, o, i):
        ts(V("CAP", 32 * t + o, 32 * t + o + count(i)), i, -1e26, OP.mult, 351.5e26, OP.add)
        ts(V("CAP", 32 * t + 16 + o, 32 * t + 16 + o + count(i)), i, 1e26, OP.mult, -351.5e26, OP.add)
        ops[-1]["skip"] = not low[t]

    def scores(t, p, n, sel, out, at):
        tr(V("TS", at, at + 32 * n), V(p, 16, 16 + 32 * n))
        tr(V("TS", at + 32 * n, at + 64 * n + 32), V(p, 0, 32 * n + 32))
        w = ind(V("TS", at, at + 64 * n + 32), sel)
        if n == 1:
            cp(out, w)
        elif low[t]:
            tt(out, w, V("CAP", 32 * t + 16, 32 * t + 32), OP.max)
        else:
            tt(out, w, V("CAP", 32 * t, 32 * t + 16), OP.min)

    own = [0 if low[t] else 12 for t in range(3)]
    SK = ["SK0", "SK1", "SK2"]
    caps(0, 0, V("PL", 0, 16))
    scores(0, "PB", 6, SEL6, V("OUT0", 0, 16), 0)
    send(0, "as0", [(V("OUT0", 0, 12), V("SK0", own[0], own[0] + 12))], [V("SK0", 12 - own[0], 24 - own[0])])
    iota(V("M", 0, 848), [[1, 848]], 176)
    tt(V("SK0", own[0], own[0] + 12), V("OUT0", 0, 12), V("CAP", 0, 12), OP.min)
    for b in range(4):
        quant("QE", "SE", 128 * b, 128, V("EYE", 3 - b, 515 - b))

    def decode(p, rc, rs, ra, n, skip, m, t, at):
        for b in range(4):
            mm(p, b, "QE", "SE", 128 * b, rc, rs, ra, n)
            cp(V("D%d" % t, DW[t] * b + at, DW[t] * b + at + m), V(p, 512 * b + skip, 512 * b + skip + m))

    cp(V("ROW", 320, 384), ind(L1, V("OA", 0, 4)))
    cp(V("ROW", 384, 448), ind(L1, V("OB", 0, 4)))
    for b in range(4):
        mem(V("D0", DW[0] * b + 544, DW[0] * b + 560), 0.0)
    tr(V("TT", 384, 512), V("ROW", 320, 448))
    cp(V("OC", 0, 16), ind(V("TT", 384, 512), DUP))
    for k, w in enumerate((R1, R2, R3)):
        cp(V("ROW", 448 + 128 * k, 576 + 128 * k), ind(w, V("OC", 0, 8)))
    decode("PB", "QB0", "SB0", 0, 224, 16, 192, 0, 0)
    tr(V("TT", 512, 896), V("ROW", 448, 832))
    cp(V("OD", 0, 16), ind(V("TT", 512, 640), DUP))
    cp(V("ROW", 832, 960), ind(R3, V("OD", 0, 8)))
    tr(V("TT", 896, 1024), V("ROW", 832, 960))
    cp(V("PL", 12, 28), ind(V("TT", 384, 960), STR))
    cp(V("PL", 22, 38), ind(V("TT", 448, 1024), STR))

    def lists(t):
        f, w = V("FL", 16 * t, 16 * t + 12), lambda k, n=12: V("TMP", 240 + 48 * t + 16 * k, 240 + 48 * t + 16 * k + n)
        ts(w(0), V("FL", 16 * t + 2, 16 * t + 14), 32.0, OP.mult)
        tt(w(0), w(0), V("J", 0, 12), OP.add)
        cp(V("NO", 12 * t, 12 * t + 12), w(0))
        tt(w(1), f, V("CF", 20, 32), OP.mult)
        tt(V("TG", 144 * t, 144 * t + 144), ind(w(1), LP), V("K12", 0, 144), OP.add)
        ops[-1]["skip"] = ops[-2]["skip"] = not low[t]

    def steps(k):
        tt(V("DL", 32 * k, 32 * k + 24), V("IDS", 32 * k, 32 * k + 24), V("IDS", 32 * k + 2, 32 * k + 26), OP.subtract)
        cp(V("DB", 144 * k, 144 * k + 144), ind(V("DL", 32 * k, 32 * k + 24), LI))

    mem(V("FL", 0, 48), 0.0)
    mem(V("IDS", 0, 64), 0.0)
    ts(V("FL", 0, 12), V("PL", 0, 12), 351.5, OP.is_lt)
    ts(V("FL", 16, 18), V("PL", 0, 2), 351.5, OP.is_lt)
    ts(V("FL", 18, 28), V("PL", 12, 22), 351.5, OP.is_lt)
    ts(V("FL", 32, 36), V("PL", 0, 4), 351.5, OP.is_lt)
    ts(V("FL", 36, 44), V("PL", 22, 30), 351.5, OP.is_lt)
    cp(V("IDS", 12, 24), V("J", 0, 12))
    ts(V("IDS", 0, 12), V("LPL", 0, 12), 192.0, OP.add)
    cp(V("IDS", 44, 56), V("J", 0, 12))
    ts(V("IDS", 32, 34), V("J", 0, 2), 368.0, OP.add)
    ts(V("IDS", 34, 44), V("J", 2, 12), 176.0, OP.add)
    for t in range(3):
        lists(t)
    steps(0)
    steps(1)
    for t in range(4):
        ts(V("XO2", 20 * t, 20 * t + 18), V("PL", 12, 30), 4.0, OP.mult, float(t), OP.add)
    for n in ("B1", "B2"):
        mem(V(n, 0, 64), 0.0)
        mem(V(n, 704, 768), 0.0)
    for t in range(4):
        cp(V("B1", 64 + t, 704, 4), ind(XW, V("XO2", 20 * t, 20 * t + 10)))
        cp(V("B2", 192 + t, 704, 4), ind(XW, V("XO2", 20 * t + 10, 20 * t + 18)))
    mem(V("BD", 0, 64), 0.0)
    mem(V("BD", 192, 512), 0.0)
    mem(V("ZC", 128, 512), 0.0)
    for t in (1, 2):
        mem(V(SK[t], 0, 32), -1e28)
        mem(V("OS%d" % t, 16, 40), 0.0)
    for b in range(4):
        mem(V("FP", FW * b + 544, FW * b + 560), 0.0)
    tt(V("TMP", 496, 498), V("J", 1, 3), V("FL", 2, 4), OP.mult)
    cp(V("OZ", 0, 2), V("TMP", 496, 498))
    caps(1, 0, V("PL", 12, 28))
    caps(2, 0, V("PL", 2, 4))
    caps(2, 2, V("PL", 22, 36))
    iota(V("VAL", 0, 32), [[1, 32]], 1024)
    iota(V("VAL", 32, 64), [[1, 32]], 32)
    iota(V("VAL", 64, 352), [[1, 288]], 1024 + 592)
    iota(V("VAL", 352, 480), [[1, 128]], 1024 + 64)
    ts(V("TMP", 384, 414), V("PL", 0, 30), 351.5, OP.is_ge)
    tt(V("TMP", 384, 414), V("TMP", 384, 414), V("J", 0, 30), OP.mult)
    tt(V("TMP", 384, 414), V("TMP", 384, 414), V("PL", 0, 30), OP.add)
    cp(V("SCO", 0, 30), V("TMP", 384, 414))
    for a, z in ((0, 16), (16, 30)):
        add("op", {"v": (50 + 16 * (z - a) * SCATTER * CY,
                         lambda q, a=a, z=z: q.tensor_copy(ap(ind(V("M", 16, 848), V("SCO", a, z))), ap(V("VAL", 16 * a, 16 * z))))},
            [V("VAL", 16 * a, 16 * z), V("SCO", a, z)], [V("M", 16, 848)])
    tr(V("MT", 0, C), V("M", 16, 16 + C))
    tr(V("MT", C, 2 * C + 32), V("M", 0, C + 32))
    cp(V("QI", 0, 32), ind(V("MT", 0, 736), V("LS", 14, 16)))
    ts(V("QI", 32, 54), V("QI", 0, 22), 10, OP.arith_shift_right)
    ts(V("QI", 64, 86), V("QI", 0, 22), 1023, OP.bitwise_and)
    ts(V("TMP", 416, 438), V("QI", 32, 54), float(CP), OP.mult)
    cp(V("FO", 0, 22), V("QI", 64, 86))
    tt(V("TMP", 448, 470), V("J", 0, 22), V("TMP", 416, 438), OP.add)
    tt(V("TMP", 470, 492), V("J", 0, 22), V("TMP", 416, 438), OP.subtract)
    cp(V("OLO", 0, 22), V("TMP", 448, 470))
    ts(V("OLO", 22, 44), V("TMP", 470, 492), float(CP), OP.add)
    for k in range(2):
        cp(V("OLR", C * k, C * k + C), ind(V("TB", 0, 2 * CP), V("OLO", 22 * k, 22 * k + 22)))
    dma("y", [V("OLR", 0, 2 * C)], [], T.ol[:], T.OLR[0:128:16, :], 2000)
    for b in range(4):
        cp(V("FP", FW * b + 192, FW * b + 544), V("XS", b, 4 * C, 4), True)
    quant("QV", "SV", 0, 128, V("VS", 0, 512))

    def fullrank(t):
        w = V(SK[t], 0, 24)
        cp(V("G1", 0, 160), ind(w, V("LT", 18, 28)))
        cp(V("G1", 160, 288), ind(w, V("LT", 28, 36)))
        tt(V("CM", 0, 288), ind(w, V("LT", 0, 18)), V("G1", 0, 288), OP.is_ge)
        scan(V("ST", 0, 288), V("D0C", 0, 288), V("CM", 0, 288))

    def place(t):
        scan(V("SC", 0, 144), V("NQ", 0, 144), V("DB", 144 * min(t, 1), 144 * min(t, 1) + 144))
        cp(V("AO", 12 * t, 12 * t + 12), V("SC", 11, 144, 12))

    tgt = lambda t: V("TG", 144 * t, 144 * t + 144) if low[t] else V("TGH", 0, 144)
    lst = lambda t: ind(V("ST", 0, 288), LSTL if low[t] else LSTH)
    took = lambda t, b, a, z: ind(V("D%d" % t, DW[t] * b, DW[t] * b + DW[t]), V("AO", 12 * t + 2 * a, 12 * t + 2 * z))
    lev = lambda n, t, b, a, z: V(n, 768 * t + 192 * b + 32 * a, 768 * t + 192 * b + 32 * z)

    def halves(n, t, b, a, z):
        ts(lev(n, t, b, a, z), took(t, b, a, z), 0.5, OP.mult)

    def means(t, b, a, z, top, o, at):
        tt(V(o, at + b, at + 128 * (z - a), 4), ind(lev("EH", t, b, 0, top), V("NO", 12 * t + 2 * a, 12 * t + 2 * z)), lev("EG", t, b, a, z), OP.add)

    def layer(t, b, a, z, p, qz, sz, at):
        mm(p, b, "QW", "SW", 128 * b, qz, sz, at, max(128, 32 * (z - a)))
        ts(lev("RL", t, b, a, z), V(p, 512 * b, 512 * b + 32 * (z - a)), 0.0, OP.max, 0.03125, OP.mult)

    def add_e(t, b, a, z, o):
        tt(o, took(t, b, a, z), lev("RL", t, b, a, z), OP.add)

    def roots(t):
        n = t + 1
        qd, sd = "QD%d" % n, "SD%d" % n
        for b in range(4):
            halves("EH", t, b, 0, 2)
            halves("EG", t, b, 0, 1)
            means(t, b, 0, 1, 2, "ZC", 0)
        quant("QZC", "SZC", 0, 128, V("ZC", 0, 512))
        for b in range(4):
            layer(t, b, 0, 1, "PB", "QZC", "SZC", 0)
            add_e(t, b, 0, 1, V("BD", 64 + b, 192, 4))
        quant(qd, sd, 0, 128, V("BD", 0, 512))
        mm("PB", 0, "QU", "SU", 0, qd, sd, 0, 128)
        send(n, "ad%d" % n, [(V(qd, 16, 48), V("QB%d" % n, 352, 384))])
        scores(n, "PB", 1, SEL1, V("OX%d" % n, 0, 16), 1120 + 96 * t)
        send(n, "ax%d" % n, [(V(sd, 16, 48), V("SB%d" % n, 352, 384)), (V("OX%d" % n, 0, 8), V("LX%d" % n, 0, 8))])
        decode("PB", qd, sd, 0, 128, 16, 32, n, 0)

    def static(t):
        b, q, s = "B%d" % t, "QB%d" % t, "SB%d" % t
        quant(q, s, 0, 192, V(b, 0, 768))
        mm("PA", 0, "QU", "SU", 0, q, s, 0, 192)
        send(t, "ac%d" % t, [(V(q, 16, 176), V(q, 192, 352))])
        scores(t, "PA", 5, SEL5, V("OS%d" % t, 0, 16), 64 + 352 * t)
        send(t, "as%d" % t, [(V(s, 16, 176), V(s, 192, 352)), (V("OS%d" % t, 0, 40), V("LS%d" % t, 0, 40))])
        tt(V(SK[t], own[t] + 2, own[t] + 12), V("OS%d" % t, 0, 10), V("CAP", 32 * t, 32 * t + 10), OP.min)

    def arrive(t):
        cp(V(SK[t], own[t], own[t] + 2), V("OX%d" % t, 0, 2))
        cp(V(SK[t], 14 - own[t], 24 - own[t]), V("LS%d" % t, 0, 10))
        fullrank(t)
        tt(V("TG2", 0, 144), lst(t), tgt(t), OP.subtract)
        mem(V("TG2", 0, 144, 12), 1.0)
        x = ind(V("LX%d" % t, 0, 8), HL)
        decode("PB", "QB%d" % t, "SB%d" % t, 256, 128, 96, 32, t, 368)
        tt(V("CC", 0, 16), x, V(SK[t], 12 - own[t], 28 - own[t]), OP.is_ge)
        tt(V("CC", 16, 32), x, V(SK[t], own[t], own[t] + 16), OP.is_gt if low[t] else OP.is_ge)
        tt(V("NQ", 0, 144), ind(V("CC", 0, 32), LC), V("TG2", 0, 144), OP.not_equal)
        place(t)

    def rest(t, a):
        for b in range(4):
            halves("EH", t, b, 2 * a, 6)
            cp(lev("EG", t, b, a, 6), lev("EH", t, b, a, 6), t < 2)
            means(t, b, a, 6, 6, "ZR", 768 * t)
        n = 192 - 32 * a
        quant("QZR", "SZR", 192 * t, n, V("ZR", 768 * t, 768 * t + 4 * n))
        for b in range(4):
            layer(t, b, a, 6, "PA", "QZR", "SZR", 192 * t)
            if t == 0:
                add_e(0, b, 1, 6, V("FP", FW * b + 560, FW * b + 720))
                cp(V("B2", 64 + b, 192, 4), ind(V("FP", FW * b + 544, FW * b + 592), V("OZ", 0, 2)))
            elif t == 1:
                add_e(1, b, 1, 6, V("FP", FW * b + 720, FW * b + 880))
            else:
                add_e(2, b, 0, 6, V("FP", FW * b, FW * b + 192))

    static(1)
    decode("PA", "LQX", "LSX", 0, C, 0, C, 0, 192)
    fullrank(0)
    tt(V("NQ", 0, 144), lst(0), tgt(0), OP.not_equal)
    ops[-1]["behind"] = [tgh]
    place(0)
    roots(0)
    decode("PB", "QB1", "SB1", 16, 336, 0, 336, 1, 32)
    rest(0, 1)
    static(2)
    arrive(1)
    roots(1)
    decode("PB", "QB2", "SB2", 16, 336, 0, 336, 2, 32)
    rest(1, 1)
    arrive(2)
    rest(2, 0)
    for b in range(4):
        for a, z in ((0, 12), (12, 22)):
            cp(V("XF", 64 * a + b, 64 * z, 4), ind(V("FP", FW * b, FW * b + FW), V("FO", a, z)))
    for k, (a, z) in enumerate(((0, 192), (192, C))):
        quant("QF", "SF", a, z - a, V("XF", 4 * a, 4 * z))
        mm("PB", k, "QV", "SV", 0, "QF", "SF", a, z - a)
        dma("y", [V("QF", a, z)], [], T.oc[:, 4 * a:4 * z], raw(V("QF", a, z)), 2000)
        cp(V("YS", a, z), V("PB", 512 * k, 512 * k + z - a))
        dma("y", [V("YS", a, z)], [], T.y[:, a:z], T.YS[:, a:z], 2000)
    for k in range(4):
        dma("sy"[k % 2], [V("SF", 0, C)], [], T.osc[4 * k:4 * k + 4, :], T.SF[32 * k:32 * k + 4, :], 2000)

    total, hist, ndma = {}, {}, 0
    known = {k: {} for k in Q}
    done = {}
    for i in lay_out(ops):
        o = ops[i]
        q = o["q"]
        if o.get("skip"):
            continue
        if o["what"] == "land":
            sem, val, clock = o["sem"], o["n"], {}
        else:
            need = {}
            met = [done[j] for j in o["after"]]
            for r, w in o["acc"]:
                met += [h[4] for h in hist.get(r[0], []) if meet(r, w, o["dma"], h[0], h[1], h[2], h[3] != q)]
            for sem, val, clock in met:
                if need.get(sem, (0, None))[0] < val:
                    need[sem] = (val, clock)
            for sem in sorted(need, key=lambda k: -len(need[k][1])):
                val, clock = need[sem]
                if known[q].get(sem, 0) < val:
                    Q[q].wait_ge(T.sem[sem], val)
                    for k in clock:
                        known[q][k] = max(known[q].get(k, 0), clock[k])
            ins = o["alt"][q][1](Q[q])
            if o["what"] == "send":
                total["sent"] = total.get("sent", 0) + o["n"]
                continue
            if o["what"] == "dma":
                sem, val = "d%d" % ndma, 16
                ndma += 1
            else:
                sem = "c" + q
                val = total.get(sem, 0) + 1
            ins.then_inc(T.sem[sem], 16 if o["what"] == "dma" else 1)
            clock = dict(known[q])
        total[sem] = val
        clock[sem] = val
        done[i] = (sem, val, clock)
        for r, w in o["acc"]:
            hist.setdefault(r[0], []).append((r, w, o["dma"], q, done[i]))
    for sem in total:
        g.wait_ge(T.sem[sem], total[sem])
